import numpy as np
import ml_dtypes


def mxq(x, axis, fmt="e4m3"):
    dtype, down = {"e4m3": (ml_dtypes.float8_e4m3fn, 7), "e5m2": (ml_dtypes.float8_e5m2, 14)}[fmt]
    v = np.moveaxis(np.asarray(x, np.float32).astype(ml_dtypes.bfloat16).astype(np.float64), axis, -1)
    blocks = v.reshape(v.shape[:-1] + (-1, 32))
    amax = np.abs(blocks).max(-1, keepdims=True)
    byte = np.maximum(np.where(amax > 0, np.frexp(amax)[1] - 1 + 127, 0) - down, 1)
    scale = np.exp2(byte - 127.0)
    codes = (blocks / scale).astype(np.float32).astype(dtype).astype(np.float64)
    return np.moveaxis((codes * scale).reshape(v.shape), -1, axis)


WIDE = False


def mx_kscale(k):
    if not WIDE:
        return np.ones(k)
    levels = np.array([30, -30])
    if k % 512:
        return np.exp2(np.random.permutation(np.resize(levels, k // 32))).repeat(32)
    a = np.empty((k // 512, 16))
    for p in range(k // 512):
        a[p, :8] = np.random.permutation(np.resize(levels, 8))
        for g in range(8):
            far = levels[np.abs(levels - a[p, g]) >= 10]
            a[p, g + 8] = far[np.random.randint(len(far))]
    return np.exp2(a.ravel()).repeat(32)


def f64(x):
    return np.asarray(x).astype(np.float64)


def striped(idx):
    return np.tile(np.asarray(idx).reshape(-1, 16).T, (8, 1)).astype(np.uint16)


def unstriped(offs):
    return offs[:16].T.reshape(-1).astype(np.int64)


def striped8(idx):
    return np.asarray(idx).reshape(8, -1, 16).transpose(0, 2, 1).reshape(128, -1).astype(np.uint16)


def unstriped8(offs):
    return offs.reshape(8, 16, -1).transpose(0, 2, 1).reshape(8, -1).astype(np.int64)


def pick8(x, idx, run):
    r = np.arange(len(x))
    return x[r[:, None], idx[r % (8 * run) // run]]


E2M1 = np.array([0.0, 0.5, 1.0, 1.5, 2.0, 3.0, 4.0, 6.0, -0.0, -0.5, -1.0, -1.5, -2.0, -3.0, -4.0, -6.0])


def pack_weight(w, fmt):
    k, n = w.shape
    w = f64(np.asarray(w, np.float32).astype(ml_dtypes.bfloat16)).reshape(k // 32, 32, n)
    amax = np.abs(w).max(1)
    if fmt in ("e4m3", "e5m2"):
        byte = np.frexp(amax)[1] - 1 + 127 - (7 if fmt == "e4m3" else 14)
    else:
        mant, ex = np.frexp(amax / 6.0)
        byte = np.where(mant > 0.5, ex, ex - 1) + 127
    byte = np.clip(np.where(amax > 0, byte, 1), 1, 254)
    scaled = (w * np.exp2(127.0 - byte)[:, None, :]).reshape(k, n).astype(np.float32)
    by_word = np.ascontiguousarray(scaled.reshape(k // 512, 128, 4, n).transpose(0, 1, 3, 2))
    if fmt in ("e4m3", "e5m2"):
        words = by_word.astype(ml_dtypes.float8_e4m3fn if fmt == "e4m3" else ml_dtypes.float8_e5m2).view(np.uint8)
    else:
        c = by_word.astype(ml_dtypes.float4_e2m1fn).view(np.uint8) & 0xF
        words = (c[..., 0::2] | (c[..., 1::2] << 4)).reshape(k // 512, 128, 2 * n)
    return np.ascontiguousarray(words), np.ascontiguousarray(byte.astype(np.uint8).reshape(k // 512, 16, n))


def unpack_weight(words, scales, fmt):
    g, _, n = scales.shape
    words = np.ascontiguousarray(words).reshape(g, 128, n, -1)
    if fmt in ("e4m3", "e5m2"):
        vals = words.view(ml_dtypes.float8_e4m3fn if fmt == "e4m3" else ml_dtypes.float8_e5m2).astype(np.float64)
    else:
        nib = np.empty((g, 128, n, 4), np.uint8)
        nib[..., 0::2] = words & 0xF
        nib[..., 1::2] = words >> 4
        vals = E2M1[nib]
    vals = vals * np.repeat(np.exp2(scales.astype(np.float64) - 127.0), 8, axis=1)[..., None]
    return vals.transpose(0, 1, 3, 2).reshape(g * 512, n)


def sigmoid(v):
    return 1.0 / (1.0 + np.exp(-v))


def sgn(shape):
    return np.random.uniform(0.5, 2.0, shape) * np.where(np.random.standard_normal(shape) < 0, -1.0, 1.0)


K, T, J, R, V, O, N, S = 512, 1024, 256, 512, 1024, 128, 256, 1024


def setup_inputs():
    n = np.random.standard_normal
    idx = np.random.permutation(V)[:R]
    idx2 = np.random.permutation(T)[:J]
    idx3 = np.stack([np.random.permutation(J)[:O] for _ in range(8)])
    idx4 = np.stack([np.random.permutation(J)[:O] for _ in range(8)])
    idx5 = np.random.permutation(S)[:N]
    fk = mx_kscale(K)
    fr = mx_kscale(R)
    xtp = pack_weight(n((K, T)) / fk[:, None], "e4m3")
    wtp = pack_weight(n((K, V)) * 1 / np.sqrt(K) * fk[:, None], "e2m1")
    vsp = pack_weight(n((R, S)) * 1 / np.sqrt(R) / fr[:, None], "e5m2")
    return {
        "xt_words": xtp[0],
        "xt_scales": xtp[1],
        "wt_words": wtp[0],
        "wt_scales": wtp[1],
        "sa": (np.random.uniform(0.5, 1.6, (R, 1)) * fr[:, None]).astype(np.float32),
        "sg": (sgn((R, 1))).astype(np.float32),
        "bg": (np.random.uniform(-2.0, 2.0, (R, 1))).astype(np.float32),
        "vs_words": vsp[0],
        "vs_scales": vsp[1],
        "offs": striped(idx),
        "offs2": striped(idx2),
        "offs3": striped8(idx3),
        "offs4": striped8(idx4),
        "offs5": striped(idx5),
    }


def reference(xt_words, xt_scales, wt_words, wt_scales, sa, sg, bg, vs_words, vs_scales, offs, offs2, offs3, offs4, offs5):
    idx = unstriped(offs)
    idx2 = unstriped(offs2)
    idx3 = unstriped8(offs3)
    idx4 = unstriped8(offs4)
    idx5 = unstriped(offs5)
    xtu = unpack_weight(xt_words, xt_scales, "e4m3")
    wtu = unpack_weight(wt_words, wt_scales, "e2m1")
    vsu = unpack_weight(vs_words, vs_scales, "e5m2")
    wtidxg = wtu[:, idx]
    xtidx2g = xtu[:, idx2]
    a = wtidxg.T @ xtidx2g
    hid = pick8(a, idx3, 64) * f64(sa) * sigmoid(pick8(a, idx4, 64) * f64(sg) + f64(bg))
    vsidx5g = vsu[:, idx5]
    hidq = mxq(hid, 0, "e4m3")
    y = vsidx5g.T @ hidq
    return y

@@ -1,0 +1,173 @@
+from contextlib import ExitStack
+
+import concourse.mybir as mybir
+
+K, T, J, R, V, O, N, S = 512, 1024, 256, 512, 1024, 128, 256, 1024
+FLOPS = 2 * K * R * J + 2 * R * N * O
+
+F32 = mybir.dt.float32
+BF16 = mybir.dt.bfloat16
+I32 = mybir.dt.int32
+U32 = mybir.dt.uint32
+U16 = mybir.dt.uint16
+U8 = mybir.dt.uint8
+E4M3 = mybir.dt.float8_e4m3fn_x4
+E5M2 = mybir.dt.float8_e5m2_x4
+E2M1 = mybir.dt.float4_e2m1fn_x4
+ACT = mybir.ActivationFunctionType
+MULT = mybir.AluOpType.mult
+
+P = 128
+PACK = 4
+HALF = O // 2
+
+
+def load_scale_rows(queue, window, scales):
+    for q in range(4):
+        queue.dma_start(out=window[32 * q : 32 * q + 4, :].bitcast(I32), in_=scales[0, 4 * q : 4 * q + 4, :].bitcast(I32))
+
+
+def tile_list_groupgated_chosen_store_plain_kernel(
+    tc, xt_words, xt_scales, wt_words, wt_scales, sa, sg, bg, vs_words, vs_scales, offs, offs2, offs3, offs4, offs5, out
+):
+    nc = tc.nc
+    with ExitStack() as ctx:
+        lists = ctx.enter_context(tc.tile_pool(name="lists", bufs=1))
+        sb = ctx.enter_context(tc.tile_pool(name="sb", bufs=1))
+        psum = ctx.enter_context(tc.psum_pool(name="psum", bufs=1))
+
+        l_wt = lists.tile([P, R // 16], U16, name="l_wt")
+        l_xt = lists.tile([P, J // 16], U16, name="l_xt")
+        l_val = lists.tile([P, O // 16], U16, name="l_val")
+        l_gate = lists.tile([P, O // 16], U16, name="l_gate")
+        l_vs = lists.tile([P, N // 16], U16, name="l_vs")
+
+        wt_w = sb.tile([P, V], U16, name="wt_w", tag="store_words", align_bytes=64)
+        xt_w = sb.tile([P, T], U32, name="xt_w", tag="xt_w", align_bytes=64)
+        wt_s = sb.tile([P, V], U8, name="wt_s", align_bytes=64)
+        xt_s = sb.tile([P, T], U8, name="xt_s", tag="xt_s", align_bytes=64)
+        vs_s = sb.tile([P, S], U8, name="vs_s", tag="vs_s", align_bytes=64)
+        sa_t = sb.tile([P, PACK], F32, name="sa_t")
+        sg_t = sb.tile([P, PACK], F32, name="sg_t")
+        bg_t = sb.tile([P, PACK], F32, name="bg_t")
+
+        nc.vector.memset(wt_s[:].bitcast(I32), 0)
+        nc.vector.memset(xt_s[:].bitcast(I32), 0)
+
+        nc.sync.dma_start(l_wt[:], offs)
+        nc.scalar.dma_start(out=wt_w[:].bitcast(I32), in_=wt_words[0].bitcast(I32))
+        load_scale_rows(nc.sync, wt_s, wt_scales)
+        nc.sync.dma_start(l_xt[:], offs2)
+        nc.sync.dma_start(out=xt_w[:].bitcast(I32), in_=xt_words[0].rearrange("p n t -> p (n t)").bitcast(I32))
+        load_scale_rows(nc.sync, xt_s, xt_scales)
+        nc.sync.dma_start(l_gate[:], offs4)
+        nc.sync.dma_start(l_val[:], offs3)
+        for queue, tile, vec in ((nc.gpsimd, sg_t, sg), (nc.gpsimd, bg_t, bg), (nc.sync, sa_t, sa)):
+            queue.dma_start(out=tile[:], in_=vec.rearrange("(p t) o -> p (t o)", t=PACK))
+        nc.sync.dma_start(l_vs[:], offs5)
+        nc.gpsimd.memset(vs_s[:].bitcast(I32), 0)
+
+        wt_gw = sb.tile([P, R], U16, name="wt_gw", align_bytes=64)
+        wt_gs = sb.tile([P, R], U8, name="wt_gs", align_bytes=64)
+        xt_gw = sb.tile([P, J], U32, name="xt_gw", tag="picked_words", align_bytes=64)
+        xt_gs = sb.tile([P, J], U8, name="xt_gs", tag="picked_scales", align_bytes=64)
+
+        nc.vector.tensor_copy(wt_gw[:], wt_w[:].indirect(l_wt[:]))
+        nc.vector.tensor_copy(wt_gs[:].rearrange("p (t m) -> p m t", t=PACK), wt_s[:].indirect(l_wt[:]))
+        nc.vector.tensor_copy(xt_gw[:], xt_w[:].indirect(l_xt[:]))
+        by_slot = wt_gw[:].rearrange("p (m t) -> p t m", t=PACK)
+        first_slot = sb.tile([P, P], U16, name="first_slot", tag="xt_w", align_bytes=64)
+        nc.vector.tensor_copy(first_slot[:], by_slot[:, 0, :])
+        nc.vector.tensor_copy(xt_gs[:], xt_s[:].indirect(l_xt[:]))
+        later_slots = sb.tile([P, PACK - 1, P], U16, name="later_slots", tag="xt_s", align_bytes=64)
+        nc.vector.tensor_copy(
+            later_slots[:].rearrange("p t (u m) -> p u t m", u=2), by_slot[:, 1:PACK, :].rearrange("p t (u m) -> p u t m", u=2)
+        )
+        wt_dealt = [first_slot[:]] + [later_slots[:, t, :] for t in range(PACK - 1)]
+
+        vs_w = sb.tile([P, S], U32, name="vs_w", tag="store_words", align_bytes=64)
+        nc.sync.dma_start(out=vs_w[:].bitcast(I32), in_=vs_words[0].rearrange("p n t -> p (n t)").bitcast(I32))
+        load_scale_rows(nc.sync, vs_s, vs_scales)
+
+        value = sb.tile([P, PACK, O], F32, name="value")
+        gate = sb.tile([P, PACK, O], F32, name="gate")
+        a_rows = []
+        for t in range(PACK):
+            acc = psum.tile([P, J], F32, name="acc%d" % t)
+            cols = slice(t * P, (t + 1) * P)
+            nc.tensor.matmul_mx(
+                out=acc[:],
+                lhsT=wt_dealt[t].bitcast(E2M1),
+                lhsT_scale=wt_gs[:, cols],
+                rhs=xt_gw[:].bitcast(E4M3),
+                rhs_scale=xt_gs[:],
+                start=True,
+                stop=True,
+            )
+            a_t = sb.tile([P, J], F32, name="a%d" % t)
+            nc.vector.tensor_copy(a_t[:], acc[:])
+            a_rows.append(a_t)
+
+        vs_gw = sb.tile([P, N], U32, name="vs_gw", tag="picked_words", align_bytes=64)
+        vs_gs = sb.tile([P, N], U8, name="vs_gs", tag="picked_scales", align_bytes=64)
+        nc.vector.tensor_copy(vs_gw[:], vs_w[:].indirect(l_vs[:]))
+        nc.vector.tensor_copy(vs_gs[:], vs_s[:].indirect(l_vs[:]))
+
+        def look(t, first, last):
+            places = slice(first, last)
+            entries = slice(first // 16, last // 16)
+            nc.scalar.activation(
+                out=gate[:, t, places],
+                in_=a_rows[t][:].indirect(l_gate[:, entries]),
+                func=ACT.Sigmoid,
+                bias=bg_t[:, t : t + 1],
+                scale=sg_t[:, t : t + 1],
+            )
+            nc.scalar.activation(
+                out=value[:, t, places],
+                in_=a_rows[t][:].indirect(l_val[:, entries]),
+                func=ACT.Copy,
+                scale=sa_t[:, t : t + 1],
+            )
+
+        hid = sb.tile([P, O * PACK], BF16, name="hid", tag="vs_s", align_bytes=64)
+        hid_w = sb.tile([P, O], U32, name="hid_w", align_bytes=64)
+        hid_s = sb.tile([P, O], U8, name="hid_s", align_bytes=64)
+
+        def quantise(first, last):
+            places = slice(first, last)
+            wide = slice(first * PACK, last * PACK)
+            nc.vector.tensor_tensor(
+                out=hid[:, wide].rearrange("p (c i t) -> p c t i", i=4, t=PACK),
+                in0=value[:, :, places].rearrange("p t (c i) -> p c t i", i=4),
+                in1=gate[:, :, places].rearrange("p t (c i) -> p c t i", i=4),
+                op=MULT,
+            )
+            nc.vector.quantize_mx(out=hid_w[:, places].bitcast(E4M3), scales=hid_s[:, places], in_=hid[:, wide])
+
+        for t in range(PACK - 1):
+            look(t, 0, O)
+        look(PACK - 1, 0, HALF)
+        look(PACK - 1, HALF, O)
+        quantise(0, HALF)
+        quantise(HALF, O)
+
+        for h in range(N // P):
+            cols = slice(h * P, (h + 1) * P)
+            res = psum.tile([P, O], F32, name="res%d" % h)
+            nc.tensor.matmul_mx(
+                out=res[:],
+                lhsT=vs_gw[:, cols].bitcast(E5M2),
+                lhsT_scale=vs_gs[:, cols],
+                rhs=hid_w[:].bitcast(E4M3),
+                rhs_scale=hid_s[:],
+                start=True,
+                stop=True,
+            )
+            y = sb.tile([P, O], F32, name="y%d" % h)
+            if h == 0:
+                nc.scalar.copy(y[:], res[:])
+                nc.scalar.dma_start(out=out[cols, :], in_=y[:])
+            else:
+                nc.vector.tensor_copy(y[:], res[:])
+                nc.sync.dma_start(out=out[cols, :], in_=y[:])

@@ -34,6 +34,7 @@ def tile_list_groupgated_chosen_store_plain_kernel(
     with ExitStack() as ctx:
         lists = ctx.enter_context(tc.tile_pool(name="lists", bufs=1))
         sb = ctx.enter_context(tc.tile_pool(name="sb", bufs=1))
+        shared = ctx.enter_context(tc.tile_pool(name="shared", bufs=1))
         psum = ctx.enter_context(tc.psum_pool(name="psum", bufs=1))
 
         l_wt = lists.tile([P, R // 16], U16, name="l_wt")
@@ -43,9 +44,9 @@ def tile_list_groupgated_chosen_store_plain_kernel(
         l_vs = lists.tile([P, N // 16], U16, name="l_vs")
 
         wt_w = sb.tile([P, V], U16, name="wt_w", tag="store_words", align_bytes=64)
-        xt_w = sb.tile([P, T], U32, name="xt_w", tag="xt_w", align_bytes=64)
+        xt_w = shared.tile([P, T], U32, name="xt_w", offset=2048, align_bytes=64)
         wt_s = sb.tile([P, V], U8, name="wt_s", align_bytes=64)
-        xt_s = sb.tile([P, T], U8, name="xt_s", tag="xt_s", align_bytes=64)
+        xt_s = shared.tile([P, T], U8, name="xt_s", offset=0, align_bytes=64)
         vs_s = sb.tile([P, S], U8, name="vs_s", tag="vs_s", align_bytes=64)
         sa_t = sb.tile([P, PACK], F32, name="sa_t")
         sg_t = sb.tile([P, PACK], F32, name="sg_t")
@@ -57,9 +58,9 @@ def tile_list_groupgated_chosen_store_plain_kernel(
         nc.sync.dma_start(l_wt[:], offs)
         nc.scalar.dma_start(out=wt_w[:].bitcast(I32), in_=wt_words[0].bitcast(I32))
         load_scale_rows(nc.sync, wt_s, wt_scales)
-        nc.sync.dma_start(l_xt[:], offs2)
         nc.sync.dma_start(out=xt_w[:].bitcast(I32), in_=xt_words[0].rearrange("p n t -> p (n t)").bitcast(I32))
         load_scale_rows(nc.sync, xt_s, xt_scales)
+        nc.sync.dma_start(l_xt[:], offs2)
         nc.sync.dma_start(l_gate[:], offs4)
         nc.sync.dma_start(l_val[:], offs3)
         for queue, tile, vec in ((nc.gpsimd, sg_t, sg), (nc.gpsimd, bg_t, bg), (nc.sync, sa_t, sa)):
@@ -73,17 +74,22 @@ def tile_list_groupgated_chosen_store_plain_kernel(
         xt_gs = sb.tile([P, J], U8, name="xt_gs", tag="picked_scales", align_bytes=64)
 
         nc.vector.tensor_copy(wt_gw[:], wt_w[:].indirect(l_wt[:]))
-        nc.vector.tensor_copy(wt_gs[:].rearrange("p (t m) -> p m t", t=PACK), wt_s[:].indirect(l_wt[:]))
+        nc.vector.tensor_copy(wt_gs[:], wt_s[:].indirect(l_wt[:]))
+        words_by_slot = wt_gw[:].rearrange("p (m t) -> p t m", t=PACK)
+        scales_by_slot = wt_gs[:].rearrange("p (m t) -> p t m", t=PACK)
         nc.vector.tensor_copy(xt_gw[:], xt_w[:].indirect(l_xt[:]))
-        by_slot = wt_gw[:].rearrange("p (m t) -> p t m", t=PACK)
-        first_slot = sb.tile([P, P], U16, name="first_slot", tag="xt_w", align_bytes=64)
-        nc.vector.tensor_copy(first_slot[:], by_slot[:, 0, :])
         nc.vector.tensor_copy(xt_gs[:], xt_s[:].indirect(l_xt[:]))
-        later_slots = sb.tile([P, PACK - 1, P], U16, name="later_slots", tag="xt_s", align_bytes=64)
-        nc.vector.tensor_copy(
-            later_slots[:].rearrange("p t (u m) -> p u t m", u=2), by_slot[:, 1:PACK, :].rearrange("p t (u m) -> p u t m", u=2)
-        )
-        wt_dealt = [first_slot[:]] + [later_slots[:, t, :] for t in range(PACK - 1)]
+        first_w = shared.tile([P, P], U16, name="first_w", offset=2048, align_bytes=64)
+        first_s = shared.tile([P, P], U8, name="first_s", offset=2048 + 2 * P, align_bytes=64)
+        nc.vector.tensor_copy(first_w[:], words_by_slot[:, 0, :])
+        nc.vector.tensor_copy(first_s[:], scales_by_slot[:, 0, :])
+        later_w = shared.tile([P, PACK - 1, P], U16, name="later_w", offset=0, align_bytes=64)
+        later_s = shared.tile([P, PACK - 1, P], U8, name="later_s", offset=(PACK - 1) * P * 2, align_bytes=64)
+        for first, last in ((1, 2), (2, PACK)):
+            for dealt, by_slot in ((later_w, words_by_slot), (later_s, scales_by_slot)):
+                nc.vector.tensor_copy(dealt[:, first - 1 : last - 1, :], by_slot[:, first:last, :])
+        slot_w = [first_w[:]] + [later_w[:, t, :] for t in range(PACK - 1)]
+        slot_s = [first_s[:]] + [later_s[:, t, :] for t in range(PACK - 1)]
 
         vs_w = sb.tile([P, S], U32, name="vs_w", tag="store_words", align_bytes=64)
         nc.sync.dma_start(out=vs_w[:].bitcast(I32), in_=vs_words[0].rearrange("p n t -> p (n t)").bitcast(I32))
@@ -94,11 +100,10 @@ def tile_list_groupgated_chosen_store_plain_kernel(
         a_rows = []
         for t in range(PACK):
             acc = psum.tile([P, J], F32, name="acc%d" % t)
-            cols = slice(t * P, (t + 1) * P)
             nc.tensor.matmul_mx(
                 out=acc[:],
-                lhsT=wt_dealt[t].bitcast(E2M1),
-                lhsT_scale=wt_gs[:, cols],
+                lhsT=slot_w[t].bitcast(E2M1),
+                lhsT_scale=slot_s[t],
                 rhs=xt_gw[:].bitcast(E4M3),
                 rhs_scale=xt_gs[:],
                 start=True,
@@ -134,23 +139,24 @@ def tile_list_groupgated_chosen_store_plain_kernel(
         hid_w = sb.tile([P, O], U32, name="hid_w", align_bytes=64)
         hid_s = sb.tile([P, O], U8, name="hid_s", align_bytes=64)
 
-        def quantise(first, last):
-            places = slice(first, last)
-            wide = slice(first * PACK, last * PACK)
+        hid_slots = hid[:].rearrange("p (o t) -> p o t", t=PACK)
+
+        def multiply(slots, places):
             nc.vector.tensor_tensor(
-                out=hid[:, wide].rearrange("p (c i t) -> p c t i", i=4, t=PACK),
-                in0=value[:, :, places].rearrange("p t (c i) -> p c t i", i=4),
-                in1=gate[:, :, places].rearrange("p t (c i) -> p c t i", i=4),
+                out=hid_slots[:, places, slots],
+                in0=value[:, slots, places].rearrange("p t o -> p o t"),
+                in1=gate[:, slots, places].rearrange("p t o -> p o t"),
                 op=MULT,
             )
-            nc.vector.quantize_mx(out=hid_w[:, places].bitcast(E4M3), scales=hid_s[:, places], in_=hid[:, wide])
 
-        for t in range(PACK - 1):
+        last = PACK - 1
+        for t in range(last):
             look(t, 0, O)
-        look(PACK - 1, 0, HALF)
-        look(PACK - 1, HALF, O)
-        quantise(0, HALF)
-        quantise(HALF, O)
+        multiply(slice(0, last), slice(0, O))
+        for first in (0, HALF):
+            look(last, first, first + HALF)
+            multiply(slice(last, PACK), slice(first, first + HALF))
+        nc.vector.quantize_mx(out=hid_w[:].bitcast(E4M3), scales=hid_s[:], in_=hid[:])
 
         for h in range(N // P):
             cols = slice(h * P, (h + 1) * P)

@@ -22,8 +22,8 @@ PACK = 4
 HALF = O // 2
 
 
-def load_scale_rows(queue, window, scales):
-    for q in range(4):
+def load_scale_rows(queue, window, scales, quadrants):
+    for q in quadrants:
         queue.dma_start(out=window[32 * q : 32 * q + 4, :].bitcast(I32), in_=scales[0, 4 * q : 4 * q + 4, :].bitcast(I32))
 
 
@@ -52,21 +52,26 @@ def tile_list_groupgated_chosen_store_plain_kernel(
         sg_t = sb.tile([P, PACK], F32, name="sg_t")
         bg_t = sb.tile([P, PACK], F32, name="bg_t")
 
-        nc.vector.memset(wt_s[:].bitcast(I32), 0)
+        nc.gpsimd.memset(wt_s[:].bitcast(I32), 0)
         nc.vector.memset(xt_s[:].bitcast(I32), 0)
+        nc.gpsimd.memset(vs_s[:].bitcast(I32), 0)
+
+        def load_column(tile, vec):
+            nc.sync.dma_start(out=tile[:], in_=vec.rearrange("(p t) o -> p (t o)", t=PACK))
 
         nc.sync.dma_start(l_wt[:], offs)
         nc.scalar.dma_start(out=wt_w[:].bitcast(I32), in_=wt_words[0].bitcast(I32))
-        load_scale_rows(nc.sync, wt_s, wt_scales)
+        load_scale_rows(nc.sync, wt_s, wt_scales, range(4))
+        load_scale_rows(nc.sync, xt_s, xt_scales, range(1))
         nc.sync.dma_start(out=xt_w[:].bitcast(I32), in_=xt_words[0].rearrange("p n t -> p (n t)").bitcast(I32))
-        load_scale_rows(nc.sync, xt_s, xt_scales)
+        load_scale_rows(nc.sync, xt_s, xt_scales, range(1, 4))
         nc.sync.dma_start(l_xt[:], offs2)
         nc.sync.dma_start(l_gate[:], offs4)
+        load_column(sg_t, sg)
+        load_column(bg_t, bg)
         nc.sync.dma_start(l_val[:], offs3)
-        for queue, tile, vec in ((nc.gpsimd, sg_t, sg), (nc.gpsimd, bg_t, bg), (nc.sync, sa_t, sa)):
-            queue.dma_start(out=tile[:], in_=vec.rearrange("(p t) o -> p (t o)", t=PACK))
+        load_column(sa_t, sa)
         nc.sync.dma_start(l_vs[:], offs5)
-        nc.gpsimd.memset(vs_s[:].bitcast(I32), 0)
 
         wt_gw = sb.tile([P, R], U16, name="wt_gw", align_bytes=64)
         wt_gs = sb.tile([P, R], U8, name="wt_gs", align_bytes=64)
@@ -78,11 +83,12 @@ def tile_list_groupgated_chosen_store_plain_kernel(
         words_by_slot = wt_gw[:].rearrange("p (m t) -> p t m", t=PACK)
         scales_by_slot = wt_gs[:].rearrange("p (m t) -> p t m", t=PACK)
         nc.vector.tensor_copy(xt_gw[:], xt_w[:].indirect(l_xt[:]))
-        nc.vector.tensor_copy(xt_gs[:], xt_s[:].indirect(l_xt[:]))
+        nc.vector.tensor_copy(xt_gs[:, 0:P], xt_s[:].indirect(l_xt[:, 0 : P // 16]))
         first_w = shared.tile([P, P], U16, name="first_w", offset=2048, align_bytes=64)
         first_s = shared.tile([P, P], U8, name="first_s", offset=2048 + 2 * P, align_bytes=64)
         nc.vector.tensor_copy(first_w[:], words_by_slot[:, 0, :])
         nc.vector.tensor_copy(first_s[:], scales_by_slot[:, 0, :])
+        nc.vector.tensor_copy(xt_gs[:, P:J], xt_s[:].indirect(l_xt[:, P // 16 : J // 16]))
         later_w = shared.tile([P, PACK - 1, P], U16, name="later_w", offset=0, align_bytes=64)
         later_s = shared.tile([P, PACK - 1, P], U8, name="later_s", offset=(PACK - 1) * P * 2, align_bytes=64)
         for first, last in ((1, 2), (2, PACK)):
@@ -93,24 +99,27 @@ def tile_list_groupgated_chosen_store_plain_kernel(
 
         vs_w = sb.tile([P, S], U32, name="vs_w", tag="store_words", align_bytes=64)
         nc.sync.dma_start(out=vs_w[:].bitcast(I32), in_=vs_words[0].rearrange("p n t -> p (n t)").bitcast(I32))
-        load_scale_rows(nc.sync, vs_s, vs_scales)
+        load_scale_rows(nc.sync, vs_s, vs_scales, range(4))
 
         value = sb.tile([P, PACK, O], F32, name="value")
         gate = sb.tile([P, PACK, O], F32, name="gate")
         a_rows = []
         for t in range(PACK):
-            acc = psum.tile([P, J], F32, name="acc%d" % t)
-            nc.tensor.matmul_mx(
-                out=acc[:],
-                lhsT=slot_w[t].bitcast(E2M1),
-                lhsT_scale=slot_s[t],
-                rhs=xt_gw[:].bitcast(E4M3),
-                rhs_scale=xt_gs[:],
-                start=True,
-                stop=True,
-            )
             a_t = sb.tile([P, J], F32, name="a%d" % t)
-            nc.vector.tensor_copy(a_t[:], acc[:])
+            width = P if t == 0 else J
+            for first in range(0, J, width):
+                slots = slice(first, first + width)
+                acc = psum.tile([P, width], F32, name="acc%d_%d" % (t, first))
+                nc.tensor.matmul_mx(
+                    out=acc[:],
+                    lhsT=slot_w[t].bitcast(E2M1),
+                    lhsT_scale=slot_s[t],
+                    rhs=xt_gw[:, slots].bitcast(E4M3),
+                    rhs_scale=xt_gs[:, slots],
+                    start=True,
+                    stop=True,
+                )
+                nc.vector.tensor_copy(a_t[:, slots], acc[:])
             a_rows.append(a_t)
 
         vs_gw = sb.tile([P, N], U32, name="vs_gw", tag="picked_words", align_bytes=64)

@@ -34,7 +34,6 @@ def tile_list_groupgated_chosen_store_plain_kernel(
     with ExitStack() as ctx:
         lists = ctx.enter_context(tc.tile_pool(name="lists", bufs=1))
         sb = ctx.enter_context(tc.tile_pool(name="sb", bufs=1))
-        shared = ctx.enter_context(tc.tile_pool(name="shared", bufs=1))
         psum = ctx.enter_context(tc.psum_pool(name="psum", bufs=1))
 
         l_wt = lists.tile([P, R // 16], U16, name="l_wt")
@@ -44,34 +43,34 @@ def tile_list_groupgated_chosen_store_plain_kernel(
         l_vs = lists.tile([P, N // 16], U16, name="l_vs")
 
         wt_w = sb.tile([P, V], U16, name="wt_w", tag="store_words", align_bytes=64)
-        xt_w = shared.tile([P, T], U32, name="xt_w", offset=2048, align_bytes=64)
+        xt_w = sb.tile([P, T], U32, name="xt_w", tag="xt_w", align_bytes=64)
         wt_s = sb.tile([P, V], U8, name="wt_s", align_bytes=64)
-        xt_s = shared.tile([P, T], U8, name="xt_s", offset=0, align_bytes=64)
+        xt_s = sb.tile([P, T], U8, name="xt_s", tag="xt_s", align_bytes=64)
         vs_s = sb.tile([P, S], U8, name="vs_s", tag="vs_s", align_bytes=64)
         sa_t = sb.tile([P, PACK], F32, name="sa_t")
         sg_t = sb.tile([P, PACK], F32, name="sg_t")
         bg_t = sb.tile([P, PACK], F32, name="bg_t")
 
-        nc.gpsimd.memset(wt_s[:].bitcast(I32), 0)
-        nc.vector.memset(xt_s[:].bitcast(I32), 0)
-        nc.gpsimd.memset(vs_s[:].bitcast(I32), 0)
+        nc.vector.memset(wt_s[:].bitcast(I32), 0)
+        nc.gpsimd.memset(xt_s[:].bitcast(I32), 0)
 
-        def load_column(tile, vec):
-            nc.sync.dma_start(out=tile[:], in_=vec.rearrange("(p t) o -> p (t o)", t=PACK))
+        def load_column(queue, tile, vec):
+            queue.dma_start(out=tile[:], in_=vec.rearrange("(p t) o -> p (t o)", t=PACK))
 
         nc.sync.dma_start(l_wt[:], offs)
         nc.scalar.dma_start(out=wt_w[:].bitcast(I32), in_=wt_words[0].bitcast(I32))
         load_scale_rows(nc.sync, wt_s, wt_scales, range(4))
-        load_scale_rows(nc.sync, xt_s, xt_scales, range(1))
         nc.sync.dma_start(out=xt_w[:].bitcast(I32), in_=xt_words[0].rearrange("p n t -> p (n t)").bitcast(I32))
-        load_scale_rows(nc.sync, xt_s, xt_scales, range(1, 4))
+        load_scale_rows(nc.sync, xt_s, xt_scales, range(3))
+        load_scale_rows(nc.gpsimd, xt_s, xt_scales, range(3, 4))
         nc.sync.dma_start(l_xt[:], offs2)
         nc.sync.dma_start(l_gate[:], offs4)
-        load_column(sg_t, sg)
-        load_column(bg_t, bg)
+        load_column(nc.sync, sg_t, sg)
+        load_column(nc.gpsimd, bg_t, bg)
         nc.sync.dma_start(l_val[:], offs3)
-        load_column(sa_t, sa)
+        load_column(nc.sync, sa_t, sa)
         nc.sync.dma_start(l_vs[:], offs5)
+        nc.gpsimd.memset(vs_s[:].bitcast(I32), 0)
 
         wt_gw = sb.tile([P, R], U16, name="wt_gw", align_bytes=64)
         wt_gs = sb.tile([P, R], U8, name="wt_gs", align_bytes=64)
@@ -79,23 +78,18 @@ def tile_list_groupgated_chosen_store_plain_kernel(
         xt_gs = sb.tile([P, J], U8, name="xt_gs", tag="picked_scales", align_bytes=64)
 
         nc.vector.tensor_copy(wt_gw[:], wt_w[:].indirect(l_wt[:]))
-        nc.vector.tensor_copy(wt_gs[:], wt_s[:].indirect(l_wt[:]))
-        words_by_slot = wt_gw[:].rearrange("p (m t) -> p t m", t=PACK)
-        scales_by_slot = wt_gs[:].rearrange("p (m t) -> p t m", t=PACK)
+        nc.vector.tensor_copy(wt_gs[:].rearrange("p (t m) -> p m t", t=PACK), wt_s[:].indirect(l_wt[:]))
         nc.vector.tensor_copy(xt_gw[:], xt_w[:].indirect(l_xt[:]))
-        nc.vector.tensor_copy(xt_gs[:, 0:P], xt_s[:].indirect(l_xt[:, 0 : P // 16]))
-        first_w = shared.tile([P, P], U16, name="first_w", offset=2048, align_bytes=64)
-        first_s = shared.tile([P, P], U8, name="first_s", offset=2048 + 2 * P, align_bytes=64)
+        nc.vector.tensor_copy(xt_gs[:], xt_s[:].indirect(l_xt[:]))
+        words_by_slot = wt_gw[:].rearrange("p (m t) -> p t m", t=PACK)
+        first_w = sb.tile([P, P], U16, name="first_w", tag="xt_w", align_bytes=64)
         nc.vector.tensor_copy(first_w[:], words_by_slot[:, 0, :])
-        nc.vector.tensor_copy(first_s[:], scales_by_slot[:, 0, :])
-        nc.vector.tensor_copy(xt_gs[:, P:J], xt_s[:].indirect(l_xt[:, P // 16 : J // 16]))
-        later_w = shared.tile([P, PACK - 1, P], U16, name="later_w", offset=0, align_bytes=64)
-        later_s = shared.tile([P, PACK - 1, P], U8, name="later_s", offset=(PACK - 1) * P * 2, align_bytes=64)
-        for first, last in ((1, 2), (2, PACK)):
-            for dealt, by_slot in ((later_w, words_by_slot), (later_s, scales_by_slot)):
-                nc.vector.tensor_copy(dealt[:, first - 1 : last - 1, :], by_slot[:, first:last, :])
+        later_w = sb.tile([P, PACK - 1, P], U16, name="later_w", tag="xt_s", align_bytes=64)
+        nc.vector.tensor_copy(
+            later_w[:].rearrange("p t (u m) -> p u t m", u=2),
+            words_by_slot[:, 1:PACK, :].rearrange("p t (u m) -> p u t m", u=2),
+        )
         slot_w = [first_w[:]] + [later_w[:, t, :] for t in range(PACK - 1)]
-        slot_s = [first_s[:]] + [later_s[:, t, :] for t in range(PACK - 1)]
 
         vs_w = sb.tile([P, S], U32, name="vs_w", tag="store_words", align_bytes=64)
         nc.sync.dma_start(out=vs_w[:].bitcast(I32), in_=vs_words[0].rearrange("p n t -> p (n t)").bitcast(I32))
@@ -113,7 +107,7 @@ def tile_list_groupgated_chosen_store_plain_kernel(
                 nc.tensor.matmul_mx(
                     out=acc[:],
                     lhsT=slot_w[t].bitcast(E2M1),
-                    lhsT_scale=slot_s[t],
+                    lhsT_scale=wt_gs[:, t * P : (t + 1) * P],
                     rhs=xt_gw[:, slots].bitcast(E4M3),
                     rhs_scale=xt_gs[:, slots],
                     start=True,

from contextlib import ExitStack

import concourse.mybir as mybir

K, T, J, R, V, O, N, S = 512, 1024, 256, 512, 1024, 128, 256, 1024
FLOPS = 2 * K * R * J + 2 * R * N * O

F32 = mybir.dt.float32
BF16 = mybir.dt.bfloat16
I32 = mybir.dt.int32
U32 = mybir.dt.uint32
U16 = mybir.dt.uint16
U8 = mybir.dt.uint8
E4M3 = mybir.dt.float8_e4m3fn_x4
E5M2 = mybir.dt.float8_e5m2_x4
E2M1 = mybir.dt.float4_e2m1fn_x4
ACT = mybir.ActivationFunctionType
MULT = mybir.AluOpType.mult

P = 128
PACK = 4
HALF = O // 2


def load_scale_rows(queue, window, scales, quadrants):
    for q in quadrants:
        queue.dma_start(out=window[32 * q : 32 * q + 4, :].bitcast(I32), in_=scales[0, 4 * q : 4 * q + 4, :].bitcast(I32))


def tile_list_groupgated_chosen_store_plain_kernel(
    tc, xt_words, xt_scales, wt_words, wt_scales, sa, sg, bg, vs_words, vs_scales, offs, offs2, offs3, offs4, offs5, out
):
    nc = tc.nc
    with ExitStack() as ctx:
        lists = ctx.enter_context(tc.tile_pool(name="lists", bufs=1))
        sb = ctx.enter_context(tc.tile_pool(name="sb", bufs=1))
        psum = ctx.enter_context(tc.psum_pool(name="psum", bufs=1))

        l_wt = lists.tile([P, R // 16], U16, name="l_wt")
        l_xt = lists.tile([P, J // 16], U16, name="l_xt")
        l_val = lists.tile([P, O // 16], U16, name="l_val")
        l_gate = lists.tile([P, O // 16], U16, name="l_gate")
        l_vs = lists.tile([P, N // 16], U16, name="l_vs")

        wt_w = sb.tile([P, V], U16, name="wt_w", tag="store_words", align_bytes=64)
        xt_w = sb.tile([P, T], U32, name="xt_w", tag="xt_w", align_bytes=64)
        wt_s = sb.tile([P, V], U8, name="wt_s", align_bytes=64)
        xt_s = sb.tile([P, T], U8, name="xt_s", tag="xt_s", align_bytes=64)
        vs_s = sb.tile([P, S], U8, name="vs_s", tag="vs_s", align_bytes=64)
        sa_t = sb.tile([P, PACK], F32, name="sa_t")
        sg_t = sb.tile([P, PACK], F32, name="sg_t")
        bg_t = sb.tile([P, PACK], F32, name="bg_t")

        nc.vector.memset(wt_s[:].bitcast(I32), 0)
        nc.gpsimd.memset(xt_s[:].bitcast(I32), 0)

        def load_column(queue, tile, vec):
            queue.dma_start(out=tile[:], in_=vec.rearrange("(p t) o -> p (t o)", t=PACK))

        nc.sync.dma_start(l_wt[:], offs)
        nc.scalar.dma_start(out=wt_w[:].bitcast(I32), in_=wt_words[0].bitcast(I32))
        load_scale_rows(nc.sync, wt_s, wt_scales, range(4))
        nc.sync.dma_start(out=xt_w[:].bitcast(I32), in_=xt_words[0].rearrange("p n t -> p (n t)").bitcast(I32))
        load_scale_rows(nc.sync, xt_s, xt_scales, range(3))
        load_scale_rows(nc.gpsimd, xt_s, xt_scales, range(3, 4))
        nc.sync.dma_start(l_xt[:], offs2)
        nc.sync.dma_start(l_gate[:], offs4)
        load_column(nc.sync, sg_t, sg)
        load_column(nc.gpsimd, bg_t, bg)
        nc.sync.dma_start(l_val[:], offs3)
        load_column(nc.sync, sa_t, sa)
        nc.sync.dma_start(l_vs[:], offs5)
        nc.gpsimd.memset(vs_s[:].bitcast(I32), 0)

        wt_gw = sb.tile([P, R], U16, name="wt_gw", align_bytes=64)
        wt_gs = sb.tile([P, R], U8, name="wt_gs", align_bytes=64)
        xt_gw = sb.tile([P, J], U32, name="xt_gw", tag="picked_words", align_bytes=64)
        xt_gs = sb.tile([P, J], U8, name="xt_gs", tag="picked_scales", align_bytes=64)

        nc.vector.tensor_copy(wt_gw[:], wt_w[:].indirect(l_wt[:]))
        nc.vector.tensor_copy(wt_gs[:].rearrange("p (t m) -> p m t", t=PACK), wt_s[:].indirect(l_wt[:]))
        nc.vector.tensor_copy(xt_gw[:], xt_w[:].indirect(l_xt[:]))
        nc.vector.tensor_copy(xt_gs[:], xt_s[:].indirect(l_xt[:]))
        words_by_slot = wt_gw[:].rearrange("p (m t) -> p t m", t=PACK)
        first_w = sb.tile([P, P], U16, name="first_w", tag="xt_w", align_bytes=64)
        nc.vector.tensor_copy(first_w[:], words_by_slot[:, 0, :])
        later_w = sb.tile([P, PACK - 1, P], U16, name="later_w", tag="xt_s", align_bytes=64)
        nc.vector.tensor_copy(
            later_w[:].rearrange("p t (u m) -> p u t m", u=2),
            words_by_slot[:, 1:PACK, :].rearrange("p t (u m) -> p u t m", u=2),
        )
        slot_w = [first_w[:]] + [later_w[:, t, :] for t in range(PACK - 1)]

        vs_w = sb.tile([P, S], U32, name="vs_w", tag="store_words", align_bytes=64)
        nc.sync.dma_start(out=vs_w[:].bitcast(I32), in_=vs_words[0].rearrange("p n t -> p (n t)").bitcast(I32))
        load_scale_rows(nc.sync, vs_s, vs_scales, range(4))

        value = sb.tile([P, PACK, O], F32, name="value")
        gate = sb.tile([P, PACK, O], F32, name="gate")
        a_rows = []
        for t in range(PACK):
            a_t = sb.tile([P, J], F32, name="a%d" % t)
            width = P if t == 0 else J
            for first in range(0, J, width):
                slots = slice(first, first + width)
                acc = psum.tile([P, width], F32, name="acc%d_%d" % (t, first))
                nc.tensor.matmul_mx(
                    out=acc[:],
                    lhsT=slot_w[t].bitcast(E2M1),
                    lhsT_scale=wt_gs[:, t * P : (t + 1) * P],
                    rhs=xt_gw[:, slots].bitcast(E4M3),
                    rhs_scale=xt_gs[:, slots],
                    start=True,
                    stop=True,
                )
                nc.vector.tensor_copy(a_t[:, slots], acc[:])
            a_rows.append(a_t)

        vs_gw = sb.tile([P, N], U32, name="vs_gw", tag="picked_words", align_bytes=64)
        vs_gs = sb.tile([P, N], U8, name="vs_gs", tag="picked_scales", align_bytes=64)
        nc.vector.tensor_copy(vs_gw[:], vs_w[:].indirect(l_vs[:]))
        nc.vector.tensor_copy(vs_gs[:], vs_s[:].indirect(l_vs[:]))

        def look(t, first, last):
            places = slice(first, last)
            entries = slice(first // 16, last // 16)
            nc.scalar.activation(
                out=gate[:, t, places],
                in_=a_rows[t][:].indirect(l_gate[:, entries]),
                func=ACT.Sigmoid,
                bias=bg_t[:, t : t + 1],
                scale=sg_t[:, t : t + 1],
            )
            nc.scalar.activation(
                out=value[:, t, places],
                in_=a_rows[t][:].indirect(l_val[:, entries]),
                func=ACT.Copy,
                scale=sa_t[:, t : t + 1],
            )

        hid = sb.tile([P, O * PACK], BF16, name="hid", tag="vs_s", align_bytes=64)
        hid_w = sb.tile([P, O], U32, name="hid_w", align_bytes=64)
        hid_s = sb.tile([P, O], U8, name="hid_s", align_bytes=64)

        hid_slots = hid[:].rearrange("p (o t) -> p o t", t=PACK)

        def multiply(slots, places):
            nc.vector.tensor_tensor(
                out=hid_slots[:, places, slots],
                in0=value[:, slots, places].rearrange("p t o -> p o t"),
                in1=gate[:, slots, places].rearrange("p t o -> p o t"),
                op=MULT,
            )

        last = PACK - 1
        for t in range(last):
            look(t, 0, O)
        multiply(slice(0, last), slice(0, O))
        for first in (0, HALF):
            look(last, first, first + HALF)
            multiply(slice(last, PACK), slice(first, first + HALF))
        nc.vector.quantize_mx(out=hid_w[:].bitcast(E4M3), scales=hid_s[:], in_=hid[:])

        for h in range(N // P):
            cols = slice(h * P, (h + 1) * P)
            res = psum.tile([P, O], F32, name="res%d" % h)
            nc.tensor.matmul_mx(
                out=res[:],
                lhsT=vs_gw[:, cols].bitcast(E5M2),
                lhsT_scale=vs_gs[:, cols],
                rhs=hid_w[:].bitcast(E4M3),
                rhs_scale=hid_s[:],
                start=True,
                stop=True,
            )
            y = sb.tile([P, O], F32, name="y%d" % h)
            if h == 0:
                nc.scalar.copy(y[:], res[:])
                nc.scalar.dma_start(out=out[cols, :], in_=y[:])
            else:
                nc.vector.tensor_copy(y[:], res[:])
                nc.sync.dma_start(out=out[cols, :], in_=y[:])
